import numpy as np
import ml_dtypes


def mxq(x, axis, fmt="e4m3"):
    dtype, down = {"e4m3": (ml_dtypes.float8_e4m3fn, 7), "e5m2": (ml_dtypes.float8_e5m2, 14)}[fmt]
    v = np.moveaxis(np.asarray(x, np.float32).astype(ml_dtypes.bfloat16).astype(np.float64), axis, -1)
    blocks = v.reshape(v.shape[:-1] + (-1, 32))
    amax = np.abs(blocks).max(-1, keepdims=True)
    byte = np.maximum(np.where(amax > 0, np.frexp(amax)[1] - 1 + 127, 0) - down, 1)
    scale = np.exp2(byte - 127.0)
    codes = (blocks / scale).astype(np.float32).astype(dtype).astype(np.float64)
    return np.moveaxis((codes * scale).reshape(v.shape), -1, axis)


WIDE = False


def mx_kscale(k):
    if not WIDE:
        return np.ones(k)
    levels = np.array([10, -10, 5, -5, 0])
    if k % 512:
        return np.exp2(np.random.permutation(np.resize(levels, k // 32))).repeat(32)
    a = np.empty((k // 512, 16))
    for p in range(k // 512):
        a[p, :8] = np.random.permutation(np.resize(levels, 8))
        for g in range(8):
            far = levels[np.abs(levels - a[p, g]) >= 10]
            a[p, g + 8] = far[np.random.randint(len(far))]
    return np.exp2(a.ravel()).repeat(32)


BF16 = ml_dtypes.bfloat16


def bf(x):
    return np.asarray(x, np.float32).astype(BF16)


def f64(x):
    return np.asarray(x).astype(np.float64)


M, K, N = 1024, 512, 2048
LAM_LO, LAM_HI = 0.7, 1.3
T1_LO, T1_HI = 0.2, 0.6
T2_LO, T2_HI = 0.1, 0.5


def soft(v, theta):
    return np.sign(v) * np.maximum(np.abs(v) - theta, 0.0)


def setup_inputs():
    s, u = mx_kscale(K), mx_kscale(M)
    return {"y": bf(np.random.standard_normal((M, K)) * s * u[:, None]),
            "enc": bf(np.random.standard_normal((K, N)) / np.sqrt(K) / s[:, None]),
            "lam": bf(np.random.uniform(LAM_LO, LAM_HI, M) * u),
            "tau1": bf(np.random.uniform(T1_LO, T1_HI, N)),
            "lat": bf(np.random.standard_normal((M, M)) / np.sqrt(M) / u),
            "inj": bf((1.0 + 0.1 * np.random.standard_normal(M)) / u),
            "tau2": bf(np.random.uniform(T2_LO, T2_HI, N))}


def reference(y, enc, lam, tau1, lat, inj, tau2):
    b = mxq(f64(y), 1, "e4m3") @ mxq(f64(enc), 0, "e4m3")
    z1 = soft(b, f64(lam)[:, None] * f64(tau1)[None, :])
    c = mxq(f64(lat), 1, "e4m3") @ mxq(z1, 0, "e4m3")
    return soft(f64(inj)[:, None] * b + c, f64(tau2)[None, :])

from contextlib import ExitStack

import concourse.mybir as mybir
from concourse.masks import make_identity

M, K, N = 1024, 512, 2048
FLOPS = 2 * M * K * N + 2 * M * M * N

F32 = mybir.dt.float32
BF16 = mybir.dt.bfloat16
U32 = mybir.dt.uint32
U8 = mybir.dt.uint8
FP8X4 = mybir.dt.float8_e4m3fn_x4
ALU = mybir.AluOpType
COPY = mybir.ActivationFunctionType.Copy

P = 128
PACK = 4
NB = 512
BLOCKS = N // NB
GROUPS = M // (P * PACK)
STEPS = BLOCKS * GROUPS
LEAD = 3


def tile_lateral_soft_threshold_layers_f4_kernel(tc, y, enc, lam, tau1, lat, inj, tau2, out):
    nc = tc.nc
    y_v = y.rearrange("(g p t) k -> g p t k", p=P, t=PACK)
    lat_v = lat.rearrange("(g p t) k -> g p t k", p=P, t=PACK)
    enc_v = enc.rearrange("(p j) n -> p j n", j=PACK)
    out_v = out.rearrange("(g p t) n -> g p t n", p=P, t=PACK)

    with ExitStack() as ctx:
        keep = ctx.enter_context(tc.tile_pool(name="keep", bufs=1))
        work = ctx.enter_context(tc.tile_pool(name="work", bufs=2))
        psum = ctx.enter_context(tc.psum_pool(name="psum", bufs=2))

        ident = keep.tile([P, P], F32, name="ident")
        make_identity(nc, ident[:])
        ident_bf = keep.tile([P, P], BF16, name="ident_bf")
        make_identity(nc, ident_bf[:])
        ones = keep.tile([P, P], BF16, name="ones")
        nc.gpsimd.memset(ones[:], 1.0)
        tau1_row = keep.tile([P, N], BF16, name="tau1_row")
        nc.vector.memset(tau1_row[:], 0.0)
        tau2_rows = keep.tile([P, P], BF16, name="tau2_rows")
        nc.gpsimd.memset(tau2_rows[:], 0.0)

        lam_in = keep.tile([P, GROUPS, PACK], BF16, name="lam_in")
        inj_in = keep.tile([P, GROUPS, PACK], BF16, name="inj_in")
        lam_c = keep.tile([P, GROUPS, PACK], F32, name="lam_c")
        nlam_c = keep.tile([P, GROUPS, PACK], F32, name="nlam_c")
        inj_c = keep.tile([P, GROUPS, PACK], F32, name="inj_c")
        tau1_bc = keep.tile([P, N], BF16, name="tau1_bc")
        tau2_c = keep.tile([P, N // P], F32, name="tau2_c")
        ntau2_c = keep.tile([P, N // P], F32, name="ntau2_c")

        y_codes = keep.tile([P, GROUPS, NB], U32, name="y_codes", align_bytes=64)
        y_scale = keep.tile([P, GROUPS, NB], U8, name="y_scale", align_bytes=64)
        enc_codes = keep.tile([P, BLOCKS, NB], U32, name="enc_codes", align_bytes=64)
        enc_scale = keep.tile([P, BLOCKS, NB], U8, name="enc_scale", align_bytes=64)
        lat_codes = keep.tile([P, GROUPS, GROUPS, NB], U32, name="lat_codes", align_bytes=64)
        lat_scale = keep.tile([P, GROUPS, GROUPS, NB], U8, name="lat_scale", align_bytes=64)

        y_sb = []
        enc_sb = []
        lat_sb = []

        def load_y(g):
            tile = work.tile([P, PACK, K], BF16, name="y_sb")
            nc.sync.dma_start(out=tile[:], in_=y_v[g])
            y_sb.append(tile)

        def load_enc(blk):
            tile = work.tile([P, PACK, NB], BF16, name="enc_sb", bufs=3)
            nc.sync.dma_start(out=tile[:], in_=enc_v[:, :, blk * NB:(blk + 1) * NB])
            enc_sb.append(tile)

        def load_lat(g):
            tile = work.tile([P, PACK, M], BF16, name="lat_sb", tag="wide")
            nc.sync.dma_start(out=tile[:], in_=lat_v[g])
            lat_sb.append(tile)

        nc.scalar.dma_start(out=tau1_row[0:1, :], in_=tau1.rearrange("(o n) -> o n", o=1))
        nc.scalar.dma_start(out=lam_in[:], in_=lam.rearrange("(g p t) -> p g t", p=P, t=PACK))
        nc.scalar.dma_start(out=inj_in[:], in_=inj.rearrange("(g p t) -> p g t", p=P, t=PACK))
        nc.scalar.dma_start(out=tau2_rows[0:N // P, :], in_=tau2.rearrange("(j p) -> j p", p=P))
        load_y(0)
        load_enc(0)
        load_y(1)
        load_enc(1)
        load_lat(0)
        load_lat(1)
        load_enc(2)

        def words_out(engine_copy, bank, dst):
            engine_copy(
                out=dst.bitcast(F32).rearrange("p (t q u) -> p t q u", t=2, u=2),
                in_=bank[:].rearrange("p (t u q) -> p t q u", t=2, u=2),
            )

        def turn(src, col0, tag, copies, name):
            grp = work.tile([P, PACK * NB], BF16, name=name, tag="grp", bufs=4, align_bytes=64)
            for half in range(2):
                bank = psum.tile([P, NB], F32, name="turned", tag=tag[half])
                for tt in range(2):
                    words = src[:, 2 * half + tt, col0:col0 + K].bitcast(F32)
                    for u in range(2):
                        slot = (2 * tt + u) * P
                        nc.tensor.transpose(bank[:, slot:slot + P], words[:, u::2], ident[:])
                words_out(copies[half], bank, grp[:, half * 1024:(half + 1) * 1024])
            return grp

        def group_enc(blk, copy):
            grp = work.tile([P, PACK * NB], BF16, name="enc_grp", tag="grp", bufs=4, align_bytes=64)
            copy(
                grp[:].rearrange("p (n j) -> p n j", j=PACK),
                enc_sb[blk][:].rearrange("p j n -> p n j"),
            )
            return grp

        def vector_copy(dst, src):
            nc.vector.tensor_copy(out=dst, in_=src)

        def scalar_copy(dst, src):
            nc.scalar.copy(out=dst, in_=src)

        def gpsimd_copy(dst, src):
            nc.gpsimd.tensor_scalar(out=dst, in0=src, scalar1=1.0, scalar2=0.0, op0=ALU.mult, op1=ALU.add)

        def quantize(grp, codes, scale):
            nc.vector.quantize_mx(out=codes.bitcast(FP8X4), scales=scale, in_=grp[:])

        def quantize_y(g, grp):
            quantize(grp, y_codes[:, g, :], y_scale[:, g, :])

        def quantize_enc(blk, grp):
            quantize(grp, enc_codes[:, blk, :], enc_scale[:, blk, :])

        def quantize_lat(h, g, grp):
            quantize(grp, lat_codes[:, h, g, :], lat_scale[:, h, g, :])

        b_ps = {}
        b_sb = {}
        ab = {}
        z_grp = {}
        z_codes = {}

        def product_b(s, t, tag):
            blk, g = divmod(s, GROUPS)
            bank = psum.tile([P, NB], F32, name="b_bank", tag=tag)
            cols = slice(t * P, (t + 1) * P)
            nc.tensor.matmul_mx(
                out=bank[:],
                lhsT=y_codes[:, g, cols].bitcast(FP8X4), lhsT_scale=y_scale[:, g, cols],
                rhs=enc_codes[:, blk, :].bitcast(FP8X4), rhs_scale=enc_scale[:, blk, :],
                start=True, stop=True,
            )
            held = work.tile([P, NB], F32, name="b_sb", bufs=18)
            nc.scalar.copy(out=held[:], in_=bank[:])
            b_ps[s, t] = bank
            b_sb[s, t] = held

        def thresholds(s, t):
            blk, g = divmod(s, GROUPS)
            if t == 0:
                ab[s] = (
                    work.tile([P, PACK, NB], F32, name="upper", bufs=3),
                    work.tile([P, PACK, NB], F32, name="lower", bufs=3),
                )
            upper, lower = ab[s]
            tau = tau1_bc[:, blk * NB:(blk + 1) * NB]
            bank = b_ps[s, t]
            nc.vector.scalar_tensor_tensor(
                out=upper[:, t, :], in0=tau, scalar=lam_c[:, g, t:t + 1], in1=bank[:], op0=ALU.mult, op1=ALU.max)
            nc.vector.scalar_tensor_tensor(
                out=lower[:, t, :], in0=tau, scalar=nlam_c[:, g, t:t + 1], in1=bank[:], op0=ALU.mult, op1=ALU.min)

        def add_z(s):
            upper, lower = ab[s]
            grp = work.tile([P, PACK * NB], BF16, name="z_grp", bufs=2, align_bytes=64)
            for piece in range(4):
                cols = slice(piece * P, (piece + 1) * P)
                nc.gpsimd.tensor_tensor(
                    out=grp[:, PACK * P * piece:PACK * P * (piece + 1)].rearrange("p (n t) -> p n t", t=PACK),
                    in0=upper[:, :, cols].rearrange("p t n -> p n t"),
                    in1=lower[:, :, cols].rearrange("p t n -> p n t"),
                    op=ALU.add,
                )
            z_grp[s] = grp

        def quantize_z(s):
            codes = work.tile([P, NB], U32, name="z_codes", bufs=4, align_bytes=64)
            scale = work.tile([P, NB], U8, name="z_scale", bufs=4, align_bytes=64)
            quantize(z_grp[s], codes[:], scale[:])
            z_codes[s] = (codes, scale)

        c_ps = {}
        e_sb = {}
        clipped = {}
        r_ps = {}
        o_sb = {}

        def product_c(s, t):
            blk, g = divmod(s, GROUPS)
            bank = psum.tile([P, NB], F32, name="c_bank", tag="c")
            cols = slice(t * P, (t + 1) * P)
            for h in range(GROUPS):
                codes, scale = z_codes[GROUPS * blk + h]
                nc.tensor.matmul_mx(
                    out=bank[:],
                    lhsT=lat_codes[:, h, g, cols].bitcast(FP8X4), lhsT_scale=lat_scale[:, h, g, cols],
                    rhs=codes[:].bitcast(FP8X4), rhs_scale=scale[:],
                    start=(h == 0), stop=(h == GROUPS - 1),
                )
            c_ps[s, t] = bank

        def excite(s, t):
            g = s % GROUPS
            if t == 0:
                e_sb[s] = work.tile([P, PACK, NB], F32, name="e_sb", tag="wide")
            nc.vector.scalar_tensor_tensor(
                out=e_sb[s][:, t, :], in0=b_sb[s, t][:], scalar=inj_c[:, g, t:t + 1], in1=c_ps[s, t][:],
                op0=ALU.mult, op1=ALU.add)

        def forward(s, j):
            bank = psum.tile([P, NB], F32, name="f_bank", tag="f")
            for t in range(PACK):
                nc.tensor.transpose(bank[:, t * P:(t + 1) * P], e_sb[s][:, t, j * P:(j + 1) * P], ident[:])
            turned = work.tile([P, NB], F32, name="e_turned", bufs=3)
            nc.scalar.copy(out=turned[:], in_=bank[:])
            col = (s // GROUPS) * PACK + j
            kappa = work.tile([P, NB], F32, name="kappa", bufs=8)
            clipped[s, j] = (turned, kappa, col)

        def clip(s, j):
            turned, kappa, col = clipped[s, j]
            nc.gpsimd.tensor_scalar(
                out=kappa[:], in0=turned[:], scalar1=tau2_c[:, col:col + 1], scalar2=ntau2_c[:, col:col + 1],
                op0=ALU.min, op1=ALU.max)

        def back(s, t):
            bank = psum.tile([P, NB], F32, name="r_bank", tag="r")
            for j in range(PACK):
                nc.tensor.transpose(bank[:, j * P:(j + 1) * P], clipped[s, j][1][:, t * P:(t + 1) * P], ident[:])
            r_ps[s, t] = bank

        def finish(s, t):
            blk, g = divmod(s, GROUPS)
            if t == 0:
                o_sb[s] = work.tile([P, PACK, NB], F32, name="o_sb")
            o = o_sb[s]
            nc.vector.tensor_tensor(
                out=o[:, t, :], in0=e_sb[s][:, t, :], in1=r_ps[s, t][:], op=ALU.subtract)
            if s == STEPS - 1 or t % 2 == 1:
                first = t if s == STEPS - 1 else t - 1
                nc.sync.dma_start(
                    out=out_v[g][:, first:t + 1, blk * NB:(blk + 1) * NB], in_=o[:, first:t + 1, :])

        def tau1_chunk(blk, tag):
            cols = slice(blk * NB, (blk + 1) * NB)
            bank = psum.tile([P, NB], F32, name="tau_bank", tag=tag)
            nc.tensor.matmul(out=bank[:], lhsT=ones[:], rhs=tau1_row[:, cols], start=True, stop=True)
            nc.scalar.copy(out=tau1_bc[:, cols], in_=bank[:])

        with tc.manual_schedule():
            nc.gpsimd.tensor_scalar(out=lam_c[:], in0=lam_in[:], scalar1=1.0, scalar2=0.0, op0=ALU.mult, op1=ALU.add)
            nc.gpsimd.tensor_scalar(out=nlam_c[:], in0=lam_in[:], scalar1=-1.0, scalar2=0.0, op0=ALU.mult, op1=ALU.add)
            nc.gpsimd.tensor_scalar(out=inj_c[:], in0=inj_in[:], scalar1=1.0, scalar2=0.0, op0=ALU.mult, op1=ALU.add)
            y0 = turn(y_sb[0], 0, ("f", "f"), (nc.vector.tensor_copy, nc.scalar.copy), "y_grp")
            tau1_chunk(0, "r")
            e0 = group_enc(0, vector_copy)
            quantize_y(0, y0)
            quantize_enc(0, e0)
            e1 = group_enc(1, gpsimd_copy)

            product_b(0, 0, "b")
            product_b(0, 1, "b")
            y1 = turn(y_sb[1], 0, ("c", "c"), (nc.scalar.copy, nc.scalar.copy), "y_grp")
            product_b(0, 2, "r")
            thresholds(0, 0)
            product_b(0, 3, "r")
            thresholds(0, 1)
            quantize_y(1, y1)
            product_b(1, 0, "b")
            product_b(1, 1, "b")
            thresholds(0, 2)
            thresholds(0, 3)
            add_z(0)
            lat00 = turn(lat_sb[0], 0, ("f", "f"), (nc.scalar.copy, nc.scalar.copy), "lat_grp")
            product_b(1, 2, "r")
            product_b(1, 3, "r")
            thresholds(1, 0)
            thresholds(1, 1)
            quantize_enc(1, e1)
            tau1_chunk(1, "c")
            lat10 = turn(lat_sb[0], K, ("f", "f"), (nc.scalar.copy, nc.scalar.copy), "lat_grp")
            product_b(2, 0, "b")
            product_b(2, 1, "b")
            thresholds(1, 2)
            thresholds(1, 3)
            add_z(1)
            quantize_lat(0, 0, lat00)
            product_b(2, 2, "r")
            product_b(2, 3, "r")
            thresholds(2, 0)
            thresholds(2, 1)
            quantize_lat(1, 0, lat10)
            lat01 = turn(lat_sb[1], 0, ("f", "f"), (nc.scalar.copy, nc.scalar.copy), "lat_grp")
            product_b(3, 0, "b")
            product_b(3, 1, "b")
            quantize_z(0)
            thresholds(2, 2)
            thresholds(2, 3)
            lat11 = turn(lat_sb[1], K, ("f", "f"), (nc.scalar.copy, nc.scalar.copy), "lat_grp")
            quantize_lat(0, 1, lat01)
            quantize_lat(1, 1, lat11)
            quantize_z(1)
            tau1_chunk(2, "c")
            tau1_chunk(3, "c")
            bank = psum.tile([P, NB], F32, name="tau2_bank", tag="c")
            nc.tensor.matmul(out=bank[:, 0:N // P], lhsT=tau2_rows[:], rhs=ident_bf[:, 0:N // P], start=True, stop=True)
            nc.scalar.copy(out=tau2_c[:], in_=bank[:, 0:N // P])
            nc.scalar.mul(out=ntau2_c[:], in_=bank[:, 0:N // P], mul=-1.0)
            load_enc(3)
            enc_grp = {2: group_enc(2, scalar_copy)}
            product_c(0, 0)
            product_c(0, 1)

            for i in range(STEPS):
                ahead = i + LEAD
                excite(i, 0)
                product_c(i, 2)
                excite(i, 1)
                product_c(i, 3)
                excite(i, 2)
                excite(i, 3)
                if i + 2 < STEPS:
                    add_z(i + 2)
                if i > 0:
                    back(i - 1, 0)
                    back(i - 1, 1)
                forward(i, 0)
                forward(i, 1)
                if ahead < STEPS:
                    thresholds(ahead, 0)
                    thresholds(ahead, 1)
                    product_b(ahead, 2, "b")
                forward(i, 2)
                if ahead < STEPS:
                    product_b(ahead, 3, "b")
                forward(i, 3)
                for j in range(PACK):
                    clip(i, j)
                if i > 0:
                    finish(i - 1, 0)
                    finish(i - 1, 1)
                    back(i - 1, 2)
                    back(i - 1, 3)
                    finish(i - 1, 2)
                    finish(i - 1, 3)
                if i + 2 < STEPS:
                    quantize_z(i + 2)
                if i == 0:
                    quantize_enc(2, enc_grp[2])
                if i == 1:
                    enc_grp[3] = group_enc(3, scalar_copy)
                if i == 2:
                    quantize_enc(3, enc_grp[3])
                if i + 1 < STEPS:
                    product_c(i + 1, 0)
                    product_c(i + 1, 1)
                if ahead < STEPS:
                    thresholds(ahead, 2)
                    thresholds(ahead, 3)
                if ahead + 1 < STEPS:
                    product_b(ahead + 1, 0, "b")
                    product_b(ahead + 1, 1, "b")
            for t in range(PACK):
                back(STEPS - 1, t)
                finish(STEPS - 1, t)
